import numpy as np
import ml_dtypes


def mxq(x, axis, fmt="e4m3"):
    dtype, down = {"e4m3": (ml_dtypes.float8_e4m3fn, 7), "e5m2": (ml_dtypes.float8_e5m2, 14)}[fmt]
    v = np.moveaxis(np.asarray(x, np.float32).astype(ml_dtypes.bfloat16).astype(np.float64), axis, -1)
    blocks = v.reshape(v.shape[:-1] + (-1, 32))
    amax = np.abs(blocks).max(-1, keepdims=True)
    byte = np.maximum(np.where(amax > 0, np.frexp(amax)[1] - 1 + 127, 0) - down, 1)
    scale = np.exp2(byte - 127.0)
    codes = (blocks / scale).astype(np.float32).astype(dtype).astype(np.float64)
    return np.moveaxis((codes * scale).reshape(v.shape), -1, axis)


WIDE = False


def mx_kscale(k):
    if not WIDE:
        return np.ones(k)
    levels = np.array([10, -10, 5, -5, 0])
    if k % 512:
        return np.exp2(np.random.permutation(np.resize(levels, k // 32))).repeat(32)
    a = np.empty((k // 512, 16))
    for p in range(k // 512):
        a[p, :8] = np.random.permutation(np.resize(levels, 8))
        for g in range(8):
            far = levels[np.abs(levels - a[p, g]) >= 10]
            a[p, g + 8] = far[np.random.randint(len(far))]
    return np.exp2(a.ravel()).repeat(32)


def f64(x):
    return np.asarray(x).astype(np.float64)


def striped(idx):
    return np.tile(np.asarray(idx).reshape(-1, 16).T, (8, 1)).astype(np.uint16)


def unstriped(offs):
    return offs[:16].T.reshape(-1).astype(np.int64)


E2M1 = np.array([0.0, 0.5, 1.0, 1.5, 2.0, 3.0, 4.0, 6.0, -0.0, -0.5, -1.0, -1.5, -2.0, -3.0, -4.0, -6.0])


def pack_weight(w, fmt):
    k, n = w.shape
    w = f64(np.asarray(w, np.float32).astype(ml_dtypes.bfloat16)).reshape(k // 32, 32, n)
    amax = np.abs(w).max(1)
    if fmt == "e4m3":
        byte = np.frexp(amax)[1] - 1 + 127 - 7
    else:
        mant, ex = np.frexp(amax / 6.0)
        byte = np.where(mant > 0.5, ex, ex - 1) + 127
    byte = np.clip(np.where(amax > 0, byte, 1), 1, 254)
    scaled = (w * np.exp2(127.0 - byte)[:, None, :]).reshape(k, n).astype(np.float32)
    by_word = np.ascontiguousarray(scaled.reshape(k // 512, 128, 4, n).transpose(0, 1, 3, 2))
    if fmt == "e4m3":
        words = by_word.astype(ml_dtypes.float8_e4m3fn).view(np.uint8)
    else:
        c = by_word.astype(ml_dtypes.float4_e2m1fn).view(np.uint8) & 0xF
        words = (c[..., 0::2] | (c[..., 1::2] << 4)).reshape(k // 512, 128, 2 * n)
    return np.ascontiguousarray(words), np.ascontiguousarray(byte.astype(np.uint8).reshape(k // 512, 16, n))


def unpack_weight(words, scales, fmt):
    g, _, n = scales.shape
    words = np.ascontiguousarray(words).reshape(g, 128, n, -1)
    if fmt == "e4m3":
        vals = words.view(ml_dtypes.float8_e4m3fn).astype(np.float64)
    else:
        nib = np.empty((g, 128, n, 4), np.uint8)
        nib[..., 0::2] = words & 0xF
        nib[..., 1::2] = words >> 4
        vals = E2M1[nib]
    vals = vals * np.repeat(np.exp2(scales.astype(np.float64) - 127.0), 8, axis=1)[..., None]
    return vals.transpose(0, 1, 3, 2).reshape(g * 512, n)


D, T, I, Q, E, X = 512, 2048, 512, 128, 512, 1024


def setup_inputs():
    n = np.random.standard_normal
    idx = np.random.permutation(T)[:I]
    idx2 = np.random.permutation(T)[:I]
    idx3 = np.random.permutation(X)[:I]
    fd = mx_kscale(D)
    fi = mx_kscale(I)
    keysp = pack_weight(n((D, T)) / fd[:, None], "e4m3")
    return {
        "query": (n((D, Q)) * 1.0 / np.sqrt(D) * fd[:, None]).astype(np.float32),
        "keys_words": keysp[0],
        "keys_scales": keysp[1],
        "os": (np.random.uniform(0.02, 0.08, (1, I)) * fi).astype(np.float32),
        "vals": (n((E, T))).astype(np.float32),
        "vals2": (n((E, X))).astype(np.float32),
        "vsc": (np.random.uniform(0.5, 2.0, (1, I)) / fi).astype(np.float32),
        "offs": striped(idx),
        "offs2": striped(idx2),
        "offs3": striped(idx3),
    }


def reference(query, keys_words, keys_scales, os, vals, vals2, vsc, offs, offs2, offs3):
    idx = unstriped(offs)
    idx2 = unstriped(offs2)
    idx3 = unstriped(offs3)
    keysu = unpack_weight(keys_words, keys_scales, "e4m3")
    queryq = mxq(f64(query), 0, "e4m3")
    a = queryq.T @ keysu
    w = a[:, idx] - a[:, idx2]
    wo1 = w * f64(os)
    wt1 = wo1.T
    vz = np.abs(f64(vals)[:, idx] - f64(vals2)[:, idx3]) * f64(vsc)
    vt1 = vz.T
    wt1q = mxq(wt1, 0, "e4m3")
    vt1q = mxq(vt1, 0, "e4m3")
    o = wt1q.T @ vt1q
    return o

@@ -1,0 +1,163 @@
+from contextlib import ExitStack
+
+import concourse.mybir as mybir
+from concourse.masks import make_identity
+
+D, T, I, Q, E, X = 512, 2048, 512, 128, 512, 1024
+FLOPS = 2 * D * Q * T + 2 * I * Q * E
+
+F32 = mybir.dt.float32
+BF16 = mybir.dt.bfloat16
+I32 = mybir.dt.int32
+U32 = mybir.dt.uint32
+U16 = mybir.dt.uint16
+U8 = mybir.dt.uint8
+FP8X4 = mybir.dt.float8_e4m3fn_x4
+COPY = mybir.ActivationFunctionType.Copy
+ABS = mybir.ActivationFunctionType.Abs
+MULT = mybir.AluOpType.mult
+
+P = 128
+PACK = 4
+BANK = 512
+KEY_LOADS = 2
+
+
+def tile_attend_difference_apartvalues_lean_kernel(
+    tc, query, keys_words, keys_scales, slot_factor, vals, vals2, vsc, offs, offs2, offs3, out
+):
+    nc = tc.nc
+    blocks = E // P
+    chunks = T // BANK
+
+    with ExitStack() as ctx:
+        keep = ctx.enter_context(tc.tile_pool(name="keep", bufs=1))
+        work = ctx.enter_context(tc.tile_pool(name="work", bufs=2))
+        psum = ctx.enter_context(tc.psum_pool(name="psum", bufs=2))
+
+        list1 = keep.tile([P, I // 16], U16, name="list1")
+        list2 = keep.tile([P, I // 16], U16, name="list2")
+        list3 = keep.tile([P, I // 16], U16, name="list3")
+        nc.sync.dma_start(list1[:], offs)
+        nc.sync.dma_start(list2[:], offs2)
+        nc.sync.dma_start(list3[:], offs3)
+
+        q_raw = keep.tile([P, PACK, Q], F32, name="q_raw")
+        nc.sync.dma_start(q_raw[:], query.rearrange("(p t) q -> p t q", t=PACK))
+
+        key_words = []
+        width = T // KEY_LOADS
+        for h in range(KEY_LOADS):
+            words = keep.tile([P, width], U32, name="key_words%d" % h, align_bytes=64)
+            src = keys_words[0].rearrange("p n t -> p (n t)")[:, PACK * width * h : PACK * width * (h + 1)]
+            nc.sync.dma_start(words[:].bitcast(I32), src.bitcast(I32))
+            key_words.append(words)
+
+        key_scales = keep.tile([P, BANK], U8, name="key_scales", align_bytes=64)
+        nc.vector.memset(key_scales[:].bitcast(I32), 0)
+        for quad in range(4):
+            rows = keys_scales[0, 4 * quad : 4 * quad + 4, :].rearrange("r (c n) -> c r n", c=chunks)
+            nc.scalar.dma_start(key_scales[32 * quad : 32 * quad + 16, :].bitcast(I32), rows.bitcast(I32))
+
+        os4 = keep.tile([P, PACK], F32, name="os4")
+        vsc4 = keep.tile([P, PACK], F32, name="vsc4")
+        nc.gpsimd.dma_start(os4[:], slot_factor.rearrange("o (p t) -> (o p) t", t=PACK))
+        nc.gpsimd.dma_start(vsc4[:], vsc.rearrange("o (p t) -> (o p) t", t=PACK))
+
+        first_store, second_store = [], []
+        for j in range(blocks):
+            v1 = keep.tile([P, T], F32, name="vals_%d" % j, tag="first_%d" % j, align_bytes=64)
+            v2 = keep.tile([P, X], F32, name="vals2_%d" % j, tag="second_%d" % j, align_bytes=64)
+            nc.sync.dma_start(v1[:], vals[P * j : P * (j + 1), :])
+            nc.sync.dma_start(v2[:], vals2[P * j : P * (j + 1), :])
+            first_store.append(v1)
+            second_store.append(v2)
+
+        ident = keep.tile([P, P], F32, name="ident")
+        make_identity(nc, ident[:])
+
+        def open_difference(window, offsets):
+            negated = work.tile([P, I], F32, name="negated")
+            nc.scalar.activation(negated[:], window[:].indirect(offsets[:]), COPY, scale=-1.0)
+            diff = psum.tile([P, PACK, P], F32, name="diff", bufs=3)
+            for t in range(PACK):
+                nc.tensor.matmul(
+                    diff[:, t, :], negated[:, t::PACK], ident[:], start=(t == 0), stop=False, is_transpose=True
+                )
+            return diff
+
+        def close_difference(diff, window, offsets):
+            dealt = work.tile([P, PACK, P], F32, name="dealt")
+            nc.vector.tensor_copy(dealt[:].rearrange("x t s -> x s t"), window[:].indirect(offsets[:]))
+            for t in range(PACK):
+                nc.tensor.matmul(
+                    diff[:, t, :], dealt[:, t, :], ident[:], start=False, stop=(t == PACK - 1), is_transpose=True
+                )
+
+        def quantised(grouped, name):
+            codes = work.tile([P, P], U32, name=name + "_codes", align_bytes=64)
+            scales = work.tile([P, P], U8, name=name + "_scales", align_bytes=64)
+            nc.vector.quantize_mx(codes[:].bitcast(FP8X4), scales[:], grouped[:].rearrange("p x t -> p (x t)"))
+            return codes, scales
+
+        q_grouped = work.tile([P, Q, PACK], BF16, name="q_grouped", align_bytes=64)
+        nc.vector.tensor_copy(q_grouped[:], q_raw[:].rearrange("p t q -> p q t"))
+        q_codes, q_scales = quantised(q_grouped, "q")
+
+        scores = keep.tile([P, T], F32, name="scores")
+        for c in range(chunks):
+            h, first = divmod(BANK * c, width)
+            bank = psum.tile([P, BANK], F32, name="score_bank", tag="product", bufs=4)
+            nc.tensor.matmul_mx(
+                bank[:],
+                q_codes[:].bitcast(FP8X4),
+                q_scales[:],
+                key_words[h][:, first : first + BANK].bitcast(FP8X4),
+                key_scales[4 * c : P, :],
+                start=True,
+                stop=True,
+            )
+            if c % 2 == 0:
+                nc.scalar.activation(scores[:, BANK * c : BANK * (c + 1)], bank[:], COPY)
+            else:
+                nc.vector.tensor_copy(scores[:, BANK * c : BANK * (c + 1)], bank[:])
+
+        w_diff = open_difference(scores, list2)
+        close_difference(w_diff, scores, list1)
+        v_diff = [open_difference(first_store[0], list1)]
+        close_difference(v_diff[0], second_store[0], list3)
+        w_grouped = keep.tile([P, Q, PACK], BF16, name="w_grouped", tag="second_0", align_bytes=64)
+        nc.vector.tensor_tensor(
+            w_grouped[:], w_diff[:].rearrange("p t q -> p q t"), os4[:].unsqueeze(1).to_broadcast([P, Q, PACK]), MULT
+        )
+        w_codes, w_scales = quantised(w_grouped, "w")
+
+        result = keep.tile([P, E], F32, name="result")
+        early = P * (blocks - 1)
+        early_bank = psum.tile([P, early], F32, name="early_bank", tag="product", bufs=4)
+        last_bank = psum.tile([P, P], F32, name="last_bank", tag="product", bufs=4)
+        for j in range(blocks):
+            if j + 1 < blocks:
+                v_diff.append(open_difference(first_store[j + 1], list1))
+            v_abs = keep.tile([P, P, PACK], F32, name="v_abs", tag="first_%d" % (j + 1), align_bytes=64)
+            nc.scalar.activation(v_abs[:], v_diff[j][:].rearrange("p t e -> p e t"), ABS)
+            if j + 1 < blocks:
+                close_difference(v_diff[j + 1], second_store[j + 1], list3)
+            v_grouped = keep.tile([P, P, PACK], BF16, name="v_grouped", tag="second_%d" % (j + 1), align_bytes=64)
+            nc.vector.tensor_tensor(v_grouped[:], v_abs[:], vsc4[:].unsqueeze(1).to_broadcast([P, P, PACK]), MULT)
+            v_codes, v_scales = quantised(v_grouped, "v")
+            target = early_bank[:, P * j : P * (j + 1)] if j + 1 < blocks else last_bank[:]
+            nc.tensor.matmul_mx(
+                target,
+                w_codes[:].bitcast(FP8X4),
+                w_scales[:],
+                v_codes[:].bitcast(FP8X4),
+                v_scales[:],
+                start=True,
+                stop=True,
+            )
+            if j == blocks - 2:
+                nc.scalar.activation(result[:, :early], early_bank[:], COPY)
+                nc.sync.dma_start(out[:, :early], result[:, :early])
+        nc.scalar.activation(result[:, early:], last_bank[:], COPY)
+        nc.sync.dma_start(out[:, early:], result[:, early:])

@@ -20,7 +20,8 @@ MULT = mybir.AluOpType.mult
 P = 128
 PACK = 4
 BANK = 512
-KEY_LOADS = 2
+KEY_LOADS = 1
+PIECES = 2
 
 
 def tile_attend_difference_apartvalues_lean_kernel(
@@ -35,46 +36,46 @@ def tile_attend_difference_apartvalues_lean_kernel(
         work = ctx.enter_context(tc.tile_pool(name="work", bufs=2))
         psum = ctx.enter_context(tc.psum_pool(name="psum", bufs=2))
 
-        list1 = keep.tile([P, I // 16], U16, name="list1")
-        list2 = keep.tile([P, I // 16], U16, name="list2")
-        list3 = keep.tile([P, I // 16], U16, name="list3")
-        nc.sync.dma_start(list1[:], offs)
-        nc.sync.dma_start(list2[:], offs2)
-        nc.sync.dma_start(list3[:], offs3)
-
         q_raw = keep.tile([P, PACK, Q], F32, name="q_raw")
         nc.sync.dma_start(q_raw[:], query.rearrange("(p t) q -> p t q", t=PACK))
 
-        key_words = []
         width = T // KEY_LOADS
+        key_bytes = keys_words[0].rearrange("p n t -> p (n t)")
+        key_words = [keep.tile([P, width], U32, name="key_words%d" % h, align_bytes=64) for h in range(KEY_LOADS)]
         for h in range(KEY_LOADS):
-            words = keep.tile([P, width], U32, name="key_words%d" % h, align_bytes=64)
-            src = keys_words[0].rearrange("p n t -> p (n t)")[:, PACK * width * h : PACK * width * (h + 1)]
-            nc.sync.dma_start(words[:].bitcast(I32), src.bitcast(I32))
-            key_words.append(words)
+            nc.sync.dma_start(
+                key_words[h][:].bitcast(I32), key_bytes[:, PACK * width * h : PACK * width * (h + 1)].bitcast(I32)
+            )
 
         key_scales = keep.tile([P, BANK], U8, name="key_scales", align_bytes=64)
-        nc.vector.memset(key_scales[:].bitcast(I32), 0)
+        nc.gpsimd.memset(key_scales[:].bitcast(I32), 0)
         for quad in range(4):
             rows = keys_scales[0, 4 * quad : 4 * quad + 4, :].rearrange("r (c n) -> c r n", c=chunks)
             nc.scalar.dma_start(key_scales[32 * quad : 32 * quad + 16, :].bitcast(I32), rows.bitcast(I32))
+
+        ident = keep.tile([P, P], F32, name="ident")
+        make_identity(nc, ident[:])
 
         os4 = keep.tile([P, PACK], F32, name="os4")
         vsc4 = keep.tile([P, PACK], F32, name="vsc4")
         nc.gpsimd.dma_start(os4[:], slot_factor.rearrange("o (p t) -> (o p) t", t=PACK))
         nc.gpsimd.dma_start(vsc4[:], vsc.rearrange("o (p t) -> (o p) t", t=PACK))
 
+        list1 = keep.tile([P, I // 16], U16, name="list1")
+        list2 = keep.tile([P, I // 16], U16, name="list2")
+        list3 = keep.tile([P, I // 16], U16, name="list3")
+        nc.sync.dma_start(list2[:], offs2)
+        nc.sync.dma_start(list1[:], offs)
         first_store, second_store = [], []
         for j in range(blocks):
             v1 = keep.tile([P, T], F32, name="vals_%d" % j, tag="first_%d" % j, align_bytes=64)
             v2 = keep.tile([P, X], F32, name="vals2_%d" % j, tag="second_%d" % j, align_bytes=64)
             nc.sync.dma_start(v1[:], vals[P * j : P * (j + 1), :])
+            if j == 0:
+                nc.sync.dma_start(list3[:], offs3)
             nc.sync.dma_start(v2[:], vals2[P * j : P * (j + 1), :])
             first_store.append(v1)
             second_store.append(v2)
-
-        ident = keep.tile([P, P], F32, name="ident")
-        make_identity(nc, ident[:])
 
         def open_difference(window, offsets):
             negated = work.tile([P, I], F32, name="negated")
@@ -136,15 +137,20 @@ def tile_attend_difference_apartvalues_lean_kernel(
         early = P * (blocks - 1)
         early_bank = psum.tile([P, early], F32, name="early_bank", tag="product", bufs=4)
         last_bank = psum.tile([P, P], F32, name="last_bank", tag="product", bufs=4)
+        piece = P // PIECES
+        pieces = [slice(piece * c, piece * (c + 1)) for c in range(PIECES)]
+        vsc_spread = vsc4[:].unsqueeze(1).to_broadcast([P, piece, PACK])
         for j in range(blocks):
             if j + 1 < blocks:
                 v_diff.append(open_difference(first_store[j + 1], list1))
             v_abs = keep.tile([P, P, PACK], F32, name="v_abs", tag="first_%d" % (j + 1), align_bytes=64)
-            nc.scalar.activation(v_abs[:], v_diff[j][:].rearrange("p t e -> p e t"), ABS)
+            for cols in pieces:
+                nc.scalar.activation(v_abs[:, cols, :], v_diff[j][:, :, cols].rearrange("p t e -> p e t"), ABS)
             if j + 1 < blocks:
                 close_difference(v_diff[j + 1], second_store[j + 1], list3)
             v_grouped = keep.tile([P, P, PACK], BF16, name="v_grouped", tag="second_%d" % (j + 1), align_bytes=64)
-            nc.vector.tensor_tensor(v_grouped[:], v_abs[:], vsc4[:].unsqueeze(1).to_broadcast([P, P, PACK]), MULT)
+            for cols in pieces:
+                nc.vector.tensor_tensor(v_grouped[:, cols, :], v_abs[:, cols, :], vsc_spread, MULT)
             v_codes, v_scales = quantised(v_grouped, "v")
             target = early_bank[:, P * j : P * (j + 1)] if j + 1 < blocks else last_bank[:]
             nc.tensor.matmul_mx(
@@ -160,4 +166,4 @@ def tile_attend_difference_apartvalues_lean_kernel(
                 nc.scalar.activation(result[:, :early], early_bank[:], COPY)
                 nc.sync.dma_start(out[:, :early], result[:, :early])
         nc.scalar.activation(result[:, early:], last_bank[:], COPY)
-        nc.sync.dma_start(out[:, early:], result[:, early:])
+        nc.scalar.dma_start(out[:, early:], result[:, early:])

from contextlib import ExitStack

import concourse.mybir as mybir
from concourse.masks import make_identity

D, T, I, Q, E, X = 512, 2048, 512, 128, 512, 1024
FLOPS = 2 * D * Q * T + 2 * I * Q * E

F32 = mybir.dt.float32
BF16 = mybir.dt.bfloat16
I32 = mybir.dt.int32
U32 = mybir.dt.uint32
U16 = mybir.dt.uint16
U8 = mybir.dt.uint8
FP8X4 = mybir.dt.float8_e4m3fn_x4
COPY = mybir.ActivationFunctionType.Copy
ABS = mybir.ActivationFunctionType.Abs
MULT = mybir.AluOpType.mult

P = 128
PACK = 4
BANK = 512
KEY_LOADS = 1
PIECES = 2


def tile_attend_difference_apartvalues_lean_kernel(
    tc, query, keys_words, keys_scales, slot_factor, vals, vals2, vsc, offs, offs2, offs3, out
):
    nc = tc.nc
    blocks = E // P
    chunks = T // BANK

    with ExitStack() as ctx:
        keep = ctx.enter_context(tc.tile_pool(name="keep", bufs=1))
        work = ctx.enter_context(tc.tile_pool(name="work", bufs=2))
        psum = ctx.enter_context(tc.psum_pool(name="psum", bufs=2))

        q_raw = keep.tile([P, PACK, Q], F32, name="q_raw")
        nc.sync.dma_start(q_raw[:], query.rearrange("(p t) q -> p t q", t=PACK))

        width = T // KEY_LOADS
        key_bytes = keys_words[0].rearrange("p n t -> p (n t)")
        key_words = [keep.tile([P, width], U32, name="key_words%d" % h, align_bytes=64) for h in range(KEY_LOADS)]
        for h in range(KEY_LOADS):
            nc.sync.dma_start(
                key_words[h][:].bitcast(I32), key_bytes[:, PACK * width * h : PACK * width * (h + 1)].bitcast(I32)
            )

        key_scales = keep.tile([P, BANK], U8, name="key_scales", align_bytes=64)
        nc.gpsimd.memset(key_scales[:].bitcast(I32), 0)
        for quad in range(4):
            rows = keys_scales[0, 4 * quad : 4 * quad + 4, :].rearrange("r (c n) -> c r n", c=chunks)
            nc.scalar.dma_start(key_scales[32 * quad : 32 * quad + 16, :].bitcast(I32), rows.bitcast(I32))

        ident = keep.tile([P, P], F32, name="ident")
        make_identity(nc, ident[:])

        os4 = keep.tile([P, PACK], F32, name="os4")
        vsc4 = keep.tile([P, PACK], F32, name="vsc4")
        nc.gpsimd.dma_start(os4[:], slot_factor.rearrange("o (p t) -> (o p) t", t=PACK))
        nc.gpsimd.dma_start(vsc4[:], vsc.rearrange("o (p t) -> (o p) t", t=PACK))

        list1 = keep.tile([P, I // 16], U16, name="list1")
        list2 = keep.tile([P, I // 16], U16, name="list2")
        list3 = keep.tile([P, I // 16], U16, name="list3")
        nc.sync.dma_start(list2[:], offs2)
        nc.sync.dma_start(list1[:], offs)
        first_store, second_store = [], []
        for j in range(blocks):
            v1 = keep.tile([P, T], F32, name="vals_%d" % j, tag="first_%d" % j, align_bytes=64)
            v2 = keep.tile([P, X], F32, name="vals2_%d" % j, tag="second_%d" % j, align_bytes=64)
            nc.sync.dma_start(v1[:], vals[P * j : P * (j + 1), :])
            if j == 0:
                nc.sync.dma_start(list3[:], offs3)
            nc.sync.dma_start(v2[:], vals2[P * j : P * (j + 1), :])
            first_store.append(v1)
            second_store.append(v2)

        def open_difference(window, offsets):
            negated = work.tile([P, I], F32, name="negated")
            nc.scalar.activation(negated[:], window[:].indirect(offsets[:]), COPY, scale=-1.0)
            diff = psum.tile([P, PACK, P], F32, name="diff", bufs=3)
            for t in range(PACK):
                nc.tensor.matmul(
                    diff[:, t, :], negated[:, t::PACK], ident[:], start=(t == 0), stop=False, is_transpose=True
                )
            return diff

        def close_difference(diff, window, offsets):
            dealt = work.tile([P, PACK, P], F32, name="dealt")
            nc.vector.tensor_copy(dealt[:].rearrange("x t s -> x s t"), window[:].indirect(offsets[:]))
            for t in range(PACK):
                nc.tensor.matmul(
                    diff[:, t, :], dealt[:, t, :], ident[:], start=False, stop=(t == PACK - 1), is_transpose=True
                )

        def quantised(grouped, name):
            codes = work.tile([P, P], U32, name=name + "_codes", align_bytes=64)
            scales = work.tile([P, P], U8, name=name + "_scales", align_bytes=64)
            nc.vector.quantize_mx(codes[:].bitcast(FP8X4), scales[:], grouped[:].rearrange("p x t -> p (x t)"))
            return codes, scales

        q_grouped = work.tile([P, Q, PACK], BF16, name="q_grouped", align_bytes=64)
        nc.vector.tensor_copy(q_grouped[:], q_raw[:].rearrange("p t q -> p q t"))
        q_codes, q_scales = quantised(q_grouped, "q")

        scores = keep.tile([P, T], F32, name="scores")
        for c in range(chunks):
            h, first = divmod(BANK * c, width)
            bank = psum.tile([P, BANK], F32, name="score_bank", tag="product", bufs=4)
            nc.tensor.matmul_mx(
                bank[:],
                q_codes[:].bitcast(FP8X4),
                q_scales[:],
                key_words[h][:, first : first + BANK].bitcast(FP8X4),
                key_scales[4 * c : P, :],
                start=True,
                stop=True,
            )
            if c % 2 == 0:
                nc.scalar.activation(scores[:, BANK * c : BANK * (c + 1)], bank[:], COPY)
            else:
                nc.vector.tensor_copy(scores[:, BANK * c : BANK * (c + 1)], bank[:])

        w_diff = open_difference(scores, list2)
        close_difference(w_diff, scores, list1)
        v_diff = [open_difference(first_store[0], list1)]
        close_difference(v_diff[0], second_store[0], list3)
        w_grouped = keep.tile([P, Q, PACK], BF16, name="w_grouped", tag="second_0", align_bytes=64)
        nc.vector.tensor_tensor(
            w_grouped[:], w_diff[:].rearrange("p t q -> p q t"), os4[:].unsqueeze(1).to_broadcast([P, Q, PACK]), MULT
        )
        w_codes, w_scales = quantised(w_grouped, "w")

        result = keep.tile([P, E], F32, name="result")
        early = P * (blocks - 1)
        early_bank = psum.tile([P, early], F32, name="early_bank", tag="product", bufs=4)
        last_bank = psum.tile([P, P], F32, name="last_bank", tag="product", bufs=4)
        piece = P // PIECES
        pieces = [slice(piece * c, piece * (c + 1)) for c in range(PIECES)]
        vsc_spread = vsc4[:].unsqueeze(1).to_broadcast([P, piece, PACK])
        for j in range(blocks):
            if j + 1 < blocks:
                v_diff.append(open_difference(first_store[j + 1], list1))
            v_abs = keep.tile([P, P, PACK], F32, name="v_abs", tag="first_%d" % (j + 1), align_bytes=64)
            for cols in pieces:
                nc.scalar.activation(v_abs[:, cols, :], v_diff[j][:, :, cols].rearrange("p t e -> p e t"), ABS)
            if j + 1 < blocks:
                close_difference(v_diff[j + 1], second_store[j + 1], list3)
            v_grouped = keep.tile([P, P, PACK], BF16, name="v_grouped", tag="second_%d" % (j + 1), align_bytes=64)
            for cols in pieces:
                nc.vector.tensor_tensor(v_grouped[:, cols, :], v_abs[:, cols, :], vsc_spread, MULT)
            v_codes, v_scales = quantised(v_grouped, "v")
            target = early_bank[:, P * j : P * (j + 1)] if j + 1 < blocks else last_bank[:]
            nc.tensor.matmul_mx(
                target,
                w_codes[:].bitcast(FP8X4),
                w_scales[:],
                v_codes[:].bitcast(FP8X4),
                v_scales[:],
                start=True,
                stop=True,
            )
            if j == blocks - 2:
                nc.scalar.activation(result[:, :early], early_bank[:], COPY)
                nc.sync.dma_start(out[:, :early], result[:, :early])
        nc.scalar.activation(result[:, early:], last_bank[:], COPY)
        nc.scalar.dma_start(out[:, early:], result[:, early:])
